import numpy as np
import ml_dtypes


def mxq(x, axis, fmt="e4m3"):
    dtype, down = {"e4m3": (ml_dtypes.float8_e4m3fn, 7), "e5m2": (ml_dtypes.float8_e5m2, 14)}[fmt]
    v = np.moveaxis(np.asarray(x, np.float32).astype(ml_dtypes.bfloat16).astype(np.float64), axis, -1)
    blocks = v.reshape(v.shape[:-1] + (-1, 32))
    amax = np.abs(blocks).max(-1, keepdims=True)
    byte = np.maximum(np.where(amax > 0, np.frexp(amax)[1] - 1 + 127, 0) - down, 1)
    scale = np.exp2(byte - 127.0)
    codes = (blocks / scale).astype(np.float32).astype(dtype).astype(np.float64)
    return np.moveaxis((codes * scale).reshape(v.shape), -1, axis)


WIDE = False


def mx_kscale(k):
    if not WIDE:
        return np.ones(k)
    levels = np.array([10, -10, 5, -5, 0])
    if k % 512:
        return np.exp2(np.random.permutation(np.resize(levels, k // 32))).repeat(32)
    a = np.empty((k // 512, 16))
    for p in range(k // 512):
        a[p, :8] = np.random.permutation(np.resize(levels, 8))
        for g in range(8):
            far = levels[np.abs(levels - a[p, g]) >= 10]
            a[p, g + 8] = far[np.random.randint(len(far))]
    return np.exp2(a.ravel()).repeat(32)


def f64(x):
    return np.asarray(x).astype(np.float64)


def striped(idx):
    return np.tile(idx.reshape(-1, 16).T, (8, 1)).astype(np.uint16)


def unstriped(offs):
    return offs[:16].T.reshape(-1).astype(np.int64)


def pack_weight(w):
    k, n = w.shape
    w = f64(np.asarray(w, np.float32).astype(ml_dtypes.bfloat16)).reshape(k // 32, 32, n)
    amax = np.abs(w).max(1)
    byte = np.clip(np.where(amax > 0, np.frexp(amax)[1] - 1 + 127 - 7, 1), 1, 254)
    scaled = (w * np.exp2(127.0 - byte)[:, None, :]).reshape(k, n).astype(np.float32)
    words = np.ascontiguousarray(scaled.reshape(k // 512, 128, 4, n).transpose(0, 1, 3, 2)).astype(ml_dtypes.float8_e4m3fn).view(np.uint8)
    return words, np.ascontiguousarray(byte.astype(np.uint8).reshape(k // 512, 16, n))


def unpack_weight(words, scales):
    g, p, n, _ = words.shape
    vals = np.ascontiguousarray(words).view(ml_dtypes.float8_e4m3fn).astype(np.float64) * np.repeat(np.exp2(scales.astype(np.float64) - 127.0), 8, axis=1)[..., None]
    return vals.transpose(0, 1, 3, 2).reshape(g * 512, n)


K, T, S, N, D, V = 1024, 4096, 1024, 128, 4, 256


def setup_inputs():
    n = np.random.standard_normal
    s = mx_kscale(K)[:, None]
    packed_xT = pack_weight(n((K, T)) * s)
    return {
        "x_words": packed_xT[0],
        "x_scales": packed_xT[1],
        "w1": (n((K, N)) / np.sqrt(K) / s).astype(np.float32),
        "w2": (n((K, N)) / np.sqrt(K) / s).astype(np.float32),
        "steer": (np.random.uniform(0.5, 1.5, (N, V))).astype(np.float32),
        "offs": striped(np.random.permutation(T)[:S]),
    }


def reference(x_words, x_scales, w1, w2, steer, offs):
    xq = unpack_weight(x_words, x_scales)[:, unstriped(offs)]
    na = mxq(f64(w1), 0, "e4m3").T @ xq
    aa = (na) ** 2
    ra = aa.reshape(len(aa), -1, D).mean(axis=2) + 0.1
    nb = mxq(f64(w2), 0, "e4m3").T @ xq
    bb = (nb) ** 2
    rb = bb.reshape(len(bb), -1, D).mean(axis=2) + 0.1
    ab = na * nb
    rx = ab.reshape(len(ab), -1, D).mean(axis=2)
    wa = rb - (rx * f64(steer))
    wb = ra * f64(steer) - rx
    den = wa + wb * f64(steer)
    return np.log((ra * rb - ((rx) ** 2) + 0.02) / (den + 0.05))

@@ -1,0 +1,204 @@
+from contextlib import ExitStack
+
+import concourse.mybir as mybir
+from concourse.masks import make_identity
+
+K, T, S, N, D, V = 1024, 4096, 1024, 128, 4, 256
+FLOPS = 2 * 2 * K * N * S
+
+F32 = mybir.dt.float32
+BF16 = mybir.dt.bfloat16
+I32 = mybir.dt.int32
+U32 = mybir.dt.uint32
+U16 = mybir.dt.uint16
+U8 = mybir.dt.uint8
+FP8X4 = mybir.dt.float8_e4m3fn_x4
+ACT = mybir.ActivationFunctionType
+ALU = mybir.AluOpType
+
+P = 128
+PACK = 4
+K_PASS = P * PACK
+PASSES = K // K_PASS
+HALF = S // 2
+VH = HALF // D
+
+
+def tile_picked_ymvdr_pow_p_kernel(tc, x_words, x_scales, w1, w2, steer, offs, out):
+    nc = tc.nc
+    with ExitStack() as ctx:
+        keep = ctx.enter_context(tc.tile_pool(name="keep", bufs=1))
+        psum = ctx.enter_context(tc.psum_pool(name="psum", bufs=1))
+
+        def sb(name, shape, dtype=F32):
+            return keep.tile(shape, dtype, name=name, align_bytes=64)
+
+        def bank(tag, name, shape):
+            return psum.tile(shape, F32, name=name, tag=tag)
+
+        offsets = keep.tile([P, S // 16], U16, name="offsets")
+        words = [sb("words%d" % g, [P, T], I32) for g in range(PASSES)]
+        planes = sb("planes", [P, T], U8)
+        raw = {(i, g): sb("raw%d%d" % (i, g), [P, PACK, N]) for i in range(2) for g in range(PASSES)}
+        steer_sb = sb("steer_sb", [P, V])
+        ident = sb("ident", [P, P])
+
+        def load_words(g):
+            nc.sync.dma_start(out=words[g][:], in_=x_words[g].rearrange("p c r -> p (c r)").bitcast(I32))
+
+        def load_weight(i, g):
+            rows = (w1, w2)[i][g * K_PASS : (g + 1) * K_PASS, :]
+            nc.sync.dma_start(out=raw[i, g][:], in_=rows.rearrange("(p j) m -> p j m", j=PACK))
+
+        nc.vector.memset(planes[:].bitcast(I32), 0)
+        make_identity(nc, ident[:])
+        nc.sync.dma_start(offsets[:], offs)
+        load_words(0)
+        for g in range(PASSES):
+            for r in range(4):
+                nc.sync.dma_start(
+                    out=planes[4 * g + r : P : 32, :].bitcast(I32),
+                    in_=x_scales[g, r:16:4, :].bitcast(I32),
+                )
+        load_weight(0, 0)
+        load_weight(1, 0)
+        nc.sync.dma_start(out=steer_sb[:], in_=steer)
+        load_weight(0, 1)
+        load_words(1)
+        load_weight(1, 1)
+
+        codes, wscales = {}, {}
+
+        def quantize_weight(i, g):
+            grouped = sb("grouped%d%d" % (i, g), [P, N, PACK], BF16)
+            nc.scalar.copy(
+                out=grouped[:].rearrange("p (c i) j -> p c j i", i=4),
+                in_=raw[i, g][:].rearrange("p j (c i) -> p c j i", i=4),
+            )
+            codes[i, g] = sb("codes%d%d" % (i, g), [P, N], U32)
+            wscales[i, g] = sb("wscales%d%d" % (i, g), [P, N], U8)
+            nc.vector.quantize_mx(
+                out=codes[i, g][:].bitcast(FP8X4),
+                scales=wscales[i, g][:],
+                in_=grouped[:].rearrange("p m j -> p (m j)"),
+            )
+
+        picked_scales = sb("picked_scales", [P, S], U8)
+        nc.vector.tensor_copy(out=picked_scales[:], in_=planes[:].indirect(offsets[:]))
+
+        picked = {}
+
+        def gather_words(g, h):
+            picked[g, h] = sb("picked%d%d" % (g, h), [P, HALF], U32)
+            cols = HALF // 16
+            nc.vector.tensor_copy(
+                out=picked[g, h][:],
+                in_=words[g][:].bitcast(U32).indirect(offsets[:, h * cols : (h + 1) * cols]),
+            )
+
+        acc = {(i, h): bank("acc%d%d" % (i, h), "acc%d%d" % (i, h), [P, HALF]) for i in range(2) for h in range(2)}
+
+        def multiply(i, g, h):
+            nc.tensor.matmul_mx(
+                out=acc[i, h][:],
+                lhsT=codes[i, g][:].bitcast(FP8X4),
+                lhsT_scale=wscales[i, g][:],
+                rhs=picked[g, h][:].bitcast(FP8X4),
+                rhs_scale=picked_scales[4 * g : P, h * HALF : (h + 1) * HALF],
+                start=(g == 0),
+                stop=(g == PASSES - 1),
+            )
+
+        gather_words(0, 0)
+        gather_words(0, 1)
+        quantize_weight(0, 0)
+        quantize_weight(1, 0)
+
+        steer_t = bank("r3", "steer_t", [P, 2, VH])
+        for h in range(2):
+            nc.tensor.transpose(steer_t[:, h, :], steer_sb[:, h * VH : (h + 1) * VH], ident[:])
+        twice_s = sb("twice_s", [P, 2, VH])
+        nc.scalar.activation(out=twice_s[:], in_=steer_t[:], func=ACT.Copy, scale=2.0)
+        neg_s2 = sb("neg_s2", [P, 2, VH])
+        nc.vector.scalar_tensor_tensor(
+            out=neg_s2[:], in0=steer_t[:], scalar=-0.5, in1=twice_s[:], op0=ALU.mult, op1=ALU.mult
+        )
+
+        quantize_weight(0, 1)
+        for h in range(2):
+            for i in range(2):
+                multiply(i, 0, h)
+        gather_words(1, 0)
+        quantize_weight(1, 1)
+        multiply(0, 1, 0)
+        multiply(1, 1, 0)
+        gather_words(1, 1)
+        multiply(0, 1, 1)
+        multiply(1, 1, 1)
+
+        def by_frame(tile):
+            return tile[:].rearrange("p (v d) -> p d v", d=D)
+
+        def transpose_sum(dst, terms):
+            for n, term in enumerate(terms):
+                nc.tensor.matmul(
+                    dst[:], lhsT=term, rhs=ident[:], is_transpose=True, start=(n == 0), stop=(n == len(terms) - 1)
+                )
+
+        def products(h):
+            na = sb("na%d" % h, [P, D, VH])
+            aa = sb("aa%d" % h, [P, D, VH])
+            bb = sb("bb%d" % h, [P, D, VH])
+            ab = sb("ab%d" % h, [P, D, VH])
+            nc.scalar.copy(out=na[:], in_=by_frame(acc[0, h]))
+            nc.scalar.activation(out=bb[:], in_=by_frame(acc[1, h]), func=ACT.Square, scale=0.5)
+            nc.vector.scalar_tensor_tensor(
+                out=aa[:], in0=na[:], scalar=0.25, in1=na[:], op0=ALU.mult, op1=ALU.mult
+            )
+            nc.vector.scalar_tensor_tensor(
+                out=ab[:], in0=by_frame(acc[1, h]), scalar=0.25, in1=na[:], op0=ALU.mult, op1=ALU.mult
+            )
+            return aa, bb, ab
+
+        def means(h, prods, tags):
+            sums = []
+            for name, tile, tag in zip(("maa", "mbb", "mab"), prods, tags):
+                dst = bank(tag, "%s%d" % (name, h), [P, P])
+                transpose_sum(dst, [tile[:, d, :] for d in range(D)])
+                sums.append(dst)
+            return sums
+
+        def finish(h, sums, num_tag, den_tag):
+            maa, mbb, mab = sums
+            neg_rb = sb("neg_rb%d" % h, [P, P])
+            rx2 = sb("rx2%d" % h, [P, P])
+            neg_ras2 = sb("neg_ras2%d" % h, [P, P])
+            neg_rarb = sb("neg_rarb%d" % h, [P, P])
+            rx2s = sb("rx2s%d" % h, [P, P])
+            nc.scalar.activation(out=neg_rb[:], in_=mbb[:], func=ACT.Copy, scale=-1.0, bias=-0.1)
+            nc.vector.scalar_tensor_tensor(
+                out=neg_ras2[:], in0=maa[:], scalar=0.1, in1=neg_s2[:, h, :], op0=ALU.add, op1=ALU.mult
+            )
+            nc.vector.scalar_tensor_tensor(
+                out=neg_rarb[:], in0=maa[:], scalar=0.1, in1=neg_rb[:], op0=ALU.add, op1=ALU.mult
+            )
+            nc.scalar.activation(out=rx2[:], in_=mab[:], func=ACT.Square)
+            nc.vector.tensor_tensor(out=rx2s[:], in0=mab[:], in1=twice_s[:, h, :], op=ALU.mult)
+            neg_num = bank(num_tag, "neg_num%d" % h, [P, VH])
+            neg_den = bank(den_tag, "neg_den%d" % h, [P, VH])
+            transpose_sum(neg_num, [neg_rarb[:], rx2[:]])
+            transpose_sum(neg_den, [neg_rb[:], neg_ras2[:], rx2s[:]])
+            ln_num = sb("ln_num%d" % h, [P, VH])
+            ln_den = sb("ln_den%d" % h, [P, VH])
+            nc.scalar.activation(out=ln_num[:], in_=neg_num[:], func=ACT.Ln, scale=-1.0, bias=0.02)
+            nc.scalar.activation(out=ln_den[:], in_=neg_den[:], func=ACT.Ln, scale=-1.0, bias=0.05)
+            result = sb("result%d" % h, [P, VH])
+            nc.vector.tensor_tensor(out=result[:], in0=ln_num[:], in1=ln_den[:], op=ALU.subtract)
+            nc.sync.dma_start(out=out[:, h * VH : (h + 1) * VH], in_=result[:])
+
+        prods0 = products(0)
+        sums0 = means(0, prods0, ("r0", "r1", "r2"))
+        prods1 = products(1)
+        sums1 = means(1, prods1, ("acc10", "acc01", "acc11"))
+        finish(0, sums0, "r3", "acc00")
+        finish(1, sums1, "r0", "r1")

@@ -30,42 +30,49 @@ def tile_picked_ymvdr_pow_p_kernel(tc, x_words, x_scales, w1, w2, steer, offs, o
         keep = ctx.enter_context(tc.tile_pool(name="keep", bufs=1))
         psum = ctx.enter_context(tc.psum_pool(name="psum", bufs=1))
 
-        def sb(name, shape, dtype=F32):
-            return keep.tile(shape, dtype, name=name, align_bytes=64)
+        def sb(name, shape, dtype=F32, tag=None):
+            return keep.tile(shape, dtype, name=name, tag=tag or name, align_bytes=64)
 
         def bank(tag, name, shape):
             return psum.tile(shape, F32, name=name, tag=tag)
 
         offsets = keep.tile([P, S // 16], U16, name="offsets")
         words = [sb("words%d" % g, [P, T], I32) for g in range(PASSES)]
-        planes = sb("planes", [P, T], U8)
+        rows = sb("rows", [P, T], U8)
+        planes = [sb("planes%d" % g, [P, S], U8) for g in range(PASSES)]
         raw = {(i, g): sb("raw%d%d" % (i, g), [P, PACK, N]) for i in range(2) for g in range(PASSES)}
         steer_sb = sb("steer_sb", [P, V])
         ident = sb("ident", [P, P])
 
-        def load_words(g):
-            nc.sync.dma_start(out=words[g][:], in_=x_words[g].rearrange("p c r -> p (c r)").bitcast(I32))
+        def load_words(g, c0, c1):
+            source = x_words[g].rearrange("p c r -> p (c r)").bitcast(I32)
+            nc.sync.dma_start(out=words[g][:, c0:c1], in_=source[:, c0:c1])
 
         def load_weight(i, g):
             rows = (w1, w2)[i][g * K_PASS : (g + 1) * K_PASS, :]
             nc.sync.dma_start(out=raw[i, g][:], in_=rows.rearrange("(p j) m -> p j m", j=PACK))
 
-        nc.vector.memset(planes[:].bitcast(I32), 0)
-        make_identity(nc, ident[:])
-        nc.sync.dma_start(offsets[:], offs)
-        load_words(0)
+        nc.gpsimd.memset(rows[:, 0 : T // 2].bitcast(I32), 0)
+        nc.vector.memset(rows[:, T // 2 : T].bitcast(I32), 0)
         for g in range(PASSES):
-            for r in range(4):
-                nc.sync.dma_start(
-                    out=planes[4 * g + r : P : 32, :].bitcast(I32),
-                    in_=x_scales[g, r:16:4, :].bitcast(I32),
-                )
+            nc.vector.memset(planes[g][:].bitcast(I32), 0)
+        make_identity(nc, ident[:])
+        ones = sb("ones", [P, 1])
+        nc.gpsimd.memset(ones[:], 1.0)
+        warm = sb("warm", [P, 1])
+        nc.scalar.activation(out=warm[:], in_=ones[:], func=ACT.Ln)
+        nc.sync.dma_start(offsets[:], offs)
+        load_weight(0, 1)
+        load_weight(1, 1)
+        nc.sync.dma_start(out=steer_sb[:], in_=steer)
+        nc.sync.dma_start(
+            out=rows[0:P:4, :].bitcast(I32), in_=x_scales.rearrange("g q t -> (g q) t").bitcast(I32)
+        )
+        load_words(0, 0, T)
+        load_words(1, 0, T // 2)
         load_weight(0, 0)
         load_weight(1, 0)
-        nc.sync.dma_start(out=steer_sb[:], in_=steer)
-        load_weight(0, 1)
-        load_words(1)
-        load_weight(1, 1)
+        load_words(1, T // 2, T)
 
         codes, wscales = {}, {}
 
@@ -83,8 +90,14 @@ def tile_picked_ymvdr_pow_p_kernel(tc, x_words, x_scales, w1, w2, steer, offs, o
                 in_=grouped[:].rearrange("p m j -> p (m j)"),
             )
 
-        picked_scales = sb("picked_scales", [P, S], U8)
-        nc.vector.tensor_copy(out=picked_scales[:], in_=planes[:].indirect(offsets[:]))
+        picked_rows = sb("picked_rows", [P, S], U8)
+        nc.vector.tensor_copy(out=picked_rows[:], in_=rows[:].indirect(offsets[:]))
+        for g, queue in enumerate((nc.scalar, nc.gpsimd)):
+            for r in range(4):
+                queue.dma_start(
+                    out=planes[g][r:P:32, :].bitcast(I32),
+                    in_=picked_rows[64 * g + 4 * r : 64 * (g + 1) : 16, :].bitcast(I32),
+                )
 
         picked = {}
 
@@ -104,15 +117,13 @@ def tile_picked_ymvdr_pow_p_kernel(tc, x_words, x_scales, w1, w2, steer, offs, o
                 lhsT=codes[i, g][:].bitcast(FP8X4),
                 lhsT_scale=wscales[i, g][:],
                 rhs=picked[g, h][:].bitcast(FP8X4),
-                rhs_scale=picked_scales[4 * g : P, h * HALF : (h + 1) * HALF],
+                rhs_scale=planes[g][:, h * HALF : (h + 1) * HALF],
                 start=(g == 0),
                 stop=(g == PASSES - 1),
             )
 
-        gather_words(0, 0)
-        gather_words(0, 1)
-        quantize_weight(0, 0)
-        quantize_weight(1, 0)
+        quantize_weight(0, 1)
+        quantize_weight(1, 1)
 
         steer_t = bank("r3", "steer_t", [P, 2, VH])
         for h in range(2):
@@ -124,17 +135,17 @@ def tile_picked_ymvdr_pow_p_kernel(tc, x_words, x_scales, w1, w2, steer, offs, o
             out=neg_s2[:], in0=steer_t[:], scalar=-0.5, in1=twice_s[:], op0=ALU.mult, op1=ALU.mult
         )
 
-        quantize_weight(0, 1)
-        for h in range(2):
-            for i in range(2):
+        gather_words(0, 0)
+        gather_words(0, 1)
+        for i in range(2):
+            quantize_weight(i, 0)
+            for h in range(2):
                 multiply(i, 0, h)
-        gather_words(1, 0)
-        quantize_weight(1, 1)
-        multiply(0, 1, 0)
-        multiply(1, 1, 0)
-        gather_words(1, 1)
-        multiply(0, 1, 1)
-        multiply(1, 1, 1)
+
+        for h in range(2):
+            gather_words(1, h)
+            for i in ((0, 1), (1, 0))[h]:
+                multiply(i, 1, h)
 
         def by_frame(tile):
             return tile[:].rearrange("p (v d) -> p d v", d=D)
@@ -145,49 +156,77 @@ def tile_picked_ymvdr_pow_p_kernel(tc, x_words, x_scales, w1, w2, steer, offs, o
                     dst[:], lhsT=term, rhs=ident[:], is_transpose=True, start=(n == 0), stop=(n == len(terms) - 1)
                 )
 
-        def products(h):
-            na = sb("na%d" % h, [P, D, VH])
-            aa = sb("aa%d" % h, [P, D, VH])
-            bb = sb("bb%d" % h, [P, D, VH])
-            ab = sb("ab%d" % h, [P, D, VH])
-            nc.scalar.copy(out=na[:], in_=by_frame(acc[0, h]))
-            nc.scalar.activation(out=bb[:], in_=by_frame(acc[1, h]), func=ACT.Square, scale=0.5)
-            nc.vector.scalar_tensor_tensor(
-                out=aa[:], in0=na[:], scalar=0.25, in1=na[:], op0=ALU.mult, op1=ALU.mult
-            )
-            nc.vector.scalar_tensor_tensor(
-                out=ab[:], in0=by_frame(acc[1, h]), scalar=0.25, in1=na[:], op0=ALU.mult, op1=ALU.mult
-            )
-            return aa, bb, ab
+        pairs = [slice(0, 2), slice(2, 4)]
 
-        def means(h, prods, tags):
-            sums = []
-            for name, tile, tag in zip(("maa", "mbb", "mab"), prods, tags):
-                dst = bank(tag, "%s%d" % (name, h), [P, P])
-                transpose_sum(dst, [tile[:, d, :] for d in range(D)])
-                sums.append(dst)
-            return sums
+        def cross(ab, h, na, ds):
+            nc.vector.scalar_tensor_tensor(
+                out=ab[:, ds, :],
+                in0=by_frame(acc[1, h])[:, ds, :],
+                scalar=0.25,
+                in1=na[:, ds, :],
+                op0=ALU.mult,
+                op1=ALU.mult,
+            )
 
-        def finish(h, sums, num_tag, den_tag):
-            maa, mbb, mab = sums
+        na, aa, bb, ab = [[sb("%s%d" % (name, h), [P, D, VH]) for h in range(2)] for name in ("na", "aa", "bb", "ab")]
+
+        def accumulate(dst, tile, ds):
+            for d in range(ds.start, ds.stop):
+                nc.tensor.matmul(
+                    dst[:], lhsT=tile[:, d, :], rhs=ident[:], is_transpose=True, start=(d == 0), stop=(d == D - 1)
+                )
+
+        every = slice(0, D)
+        nc.scalar.copy(out=na[0][:], in_=by_frame(acc[0, 0]))
+        nc.scalar.activation(out=bb[0][:], in_=by_frame(acc[1, 0]), func=ACT.Square, scale=0.5)
+        nc.vector.scalar_tensor_tensor(
+            out=aa[0][:], in0=by_frame(acc[0, 0]), scalar=0.25, in1=na[0][:], op0=ALU.mult, op1=ALU.mult
+        )
+        cross(ab[0], 0, na[0], every)
+        nc.scalar.activation(out=bb[1][:], in_=by_frame(acc[1, 1]), func=ACT.Square, scale=0.5)
+        nc.scalar.copy(out=na[1][:], in_=by_frame(acc[0, 1]))
+        maa0 = bank("r0", "maa0", [P, P])
+        mbb0 = bank("r1", "mbb0", [P, P])
+        mab0 = bank("r2", "mab0", [P, P])
+        accumulate(mbb0, bb[0], every)
+        accumulate(maa0, aa[0], every)
+        accumulate(mab0, ab[0], every)
+        mbb1 = bank("acc00", "mbb1", [P, P])
+        accumulate(mbb1, bb[1], every)
+        mab1 = bank("acc10", "mab1", [P, P])
+        maa1 = bank("acc01", "maa1", [P, P])
+        for ds in pairs:
+            cross(ab[1], 1, na[1], ds)
+            nc.scalar.activation(out=aa[1][:, ds, :], in_=na[1][:, ds, :], func=ACT.Square, scale=0.5)
+            accumulate(mab1, ab[1], ds)
+            accumulate(maa1, aa[1], ds)
+
+        def finish(h, maa, mbb, mab, num_tag, den_tag):
             neg_rb = sb("neg_rb%d" % h, [P, P])
             rx2 = sb("rx2%d" % h, [P, P])
             neg_ras2 = sb("neg_ras2%d" % h, [P, P])
             neg_rarb = sb("neg_rarb%d" % h, [P, P])
             rx2s = sb("rx2s%d" % h, [P, P])
-            nc.scalar.activation(out=neg_rb[:], in_=mbb[:], func=ACT.Copy, scale=-1.0, bias=-0.1)
-            nc.vector.scalar_tensor_tensor(
-                out=neg_ras2[:], in0=maa[:], scalar=0.1, in1=neg_s2[:, h, :], op0=ALU.add, op1=ALU.mult
-            )
+            if h == 0:
+                nc.vector.tensor_scalar(
+                    out=neg_rb[:], in0=mbb[:], scalar1=-1.0, scalar2=-0.1, op0=ALU.mult, op1=ALU.add
+                )
+            else:
+                nc.scalar.activation(out=neg_rb[:], in_=mbb[:], func=ACT.Copy, scale=-1.0, bias=-0.1)
+            nc.vector.tensor_tensor(out=rx2s[:], in0=mab[:], in1=twice_s[:, h, :], op=ALU.mult)
+            nc.scalar.activation(out=rx2[:], in_=mab[:], func=ACT.Square)
             nc.vector.scalar_tensor_tensor(
                 out=neg_rarb[:], in0=maa[:], scalar=0.1, in1=neg_rb[:], op0=ALU.add, op1=ALU.mult
             )
-            nc.scalar.activation(out=rx2[:], in_=mab[:], func=ACT.Square)
-            nc.vector.tensor_tensor(out=rx2s[:], in0=mab[:], in1=twice_s[:, h, :], op=ALU.mult)
+            nc.vector.scalar_tensor_tensor(
+                out=neg_ras2[:], in0=maa[:], scalar=0.1, in1=neg_s2[:, h, :], op0=ALU.add, op1=ALU.mult
+            )
             neg_num = bank(num_tag, "neg_num%d" % h, [P, VH])
             neg_den = bank(den_tag, "neg_den%d" % h, [P, VH])
-            transpose_sum(neg_num, [neg_rarb[:], rx2[:]])
-            transpose_sum(neg_den, [neg_rb[:], neg_ras2[:], rx2s[:]])
+            terms = [(neg_den, neg_rb, True, False), (neg_den, rx2s, False, False), (neg_num, rx2, True, False),
+                     (neg_num, neg_rarb, False, True), (neg_den, neg_ras2, False, True)]
+            for dst, term, first, last in terms:
+                nc.tensor.matmul(dst[:], lhsT=term[:], rhs=ident[:], is_transpose=True, start=first, stop=last)
             ln_num = sb("ln_num%d" % h, [P, VH])
             ln_den = sb("ln_den%d" % h, [P, VH])
             nc.scalar.activation(out=ln_num[:], in_=neg_num[:], func=ACT.Ln, scale=-1.0, bias=0.02)
@@ -196,9 +235,5 @@ def tile_picked_ymvdr_pow_p_kernel(tc, x_words, x_scales, w1, w2, steer, offs, o
             nc.vector.tensor_tensor(out=result[:], in0=ln_num[:], in1=ln_den[:], op=ALU.subtract)
             nc.sync.dma_start(out=out[:, h * VH : (h + 1) * VH], in_=result[:])
 
-        prods0 = products(0)
-        sums0 = means(0, prods0, ("r0", "r1", "r2"))
-        prods1 = products(1)
-        sums1 = means(1, prods1, ("acc10", "acc01", "acc11"))
-        finish(0, sums0, "r3", "acc00")
-        finish(1, sums1, "r0", "r1")
+        finish(0, maa0, mbb0, mab0, "r3", "r1")
+        finish(1, maa1, mbb1, mab1, "acc11", "r2")

@@ -22,6 +22,7 @@ K_PASS = P * PACK
 PASSES = K // K_PASS
 HALF = S // 2
 VH = HALF // D
+CLEAR = 2048
 
 
 def tile_picked_ymvdr_pow_p_kernel(tc, x_words, x_scales, w1, w2, steer, offs, out):
@@ -37,23 +38,23 @@ def tile_picked_ymvdr_pow_p_kernel(tc, x_words, x_scales, w1, w2, steer, offs, o
             return psum.tile(shape, F32, name=name, tag=tag)
 
         offsets = keep.tile([P, S // 16], U16, name="offsets")
-        words = [sb("words%d" % g, [P, T], I32) for g in range(PASSES)]
+        words = {}
         rows = sb("rows", [P, T], U8)
         planes = [sb("planes%d" % g, [P, S], U8) for g in range(PASSES)]
         raw = {(i, g): sb("raw%d%d" % (i, g), [P, PACK, N]) for i in range(2) for g in range(PASSES)}
         steer_sb = sb("steer_sb", [P, V])
         ident = sb("ident", [P, P])
 
-        def load_words(g, c0, c1):
-            source = x_words[g].rearrange("p c r -> p (c r)").bitcast(I32)
-            nc.sync.dma_start(out=words[g][:, c0:c1], in_=source[:, c0:c1])
+        def load_words(g, tag):
+            words[g] = sb("words%d" % g, [P, T], I32, tag=tag)
+            nc.sync.dma_start(out=words[g][:], in_=x_words[g].rearrange("p c r -> p (c r)").bitcast(I32))
 
         def load_weight(i, g):
             rows = (w1, w2)[i][g * K_PASS : (g + 1) * K_PASS, :]
             nc.sync.dma_start(out=raw[i, g][:], in_=rows.rearrange("(p j) m -> p j m", j=PACK))
 
-        nc.gpsimd.memset(rows[:, 0 : T // 2].bitcast(I32), 0)
-        nc.vector.memset(rows[:, T // 2 : T].bitcast(I32), 0)
+        nc.gpsimd.memset(rows[:, 0:CLEAR].bitcast(I32), 0)
+        nc.vector.memset(rows[:, CLEAR:T].bitcast(I32), 0)
         for g in range(PASSES):
             nc.vector.memset(planes[g][:].bitcast(I32), 0)
         make_identity(nc, ident[:])
@@ -62,42 +63,46 @@ def tile_picked_ymvdr_pow_p_kernel(tc, x_words, x_scales, w1, w2, steer, offs, o
         warm = sb("warm", [P, 1])
         nc.scalar.activation(out=warm[:], in_=ones[:], func=ACT.Ln)
         nc.sync.dma_start(offsets[:], offs)
-        load_weight(0, 1)
-        load_weight(1, 1)
-        nc.sync.dma_start(out=steer_sb[:], in_=steer)
+        load_weight(0, 0)
+        load_weight(1, 0)
         nc.sync.dma_start(
             out=rows[0:P:4, :].bitcast(I32), in_=x_scales.rearrange("g q t -> (g q) t").bitcast(I32)
         )
-        load_words(0, 0, T)
-        load_words(1, 0, T // 2)
-        load_weight(0, 0)
-        load_weight(1, 0)
-        load_words(1, T // 2, T)
-
-        codes, wscales = {}, {}
-
-        def quantize_weight(i, g):
-            grouped = sb("grouped%d%d" % (i, g), [P, N, PACK], BF16)
-            nc.scalar.copy(
-                out=grouped[:].rearrange("p (c i) j -> p c j i", i=4),
-                in_=raw[i, g][:].rearrange("p j (c i) -> p c j i", i=4),
-            )
-            codes[i, g] = sb("codes%d%d" % (i, g), [P, N], U32)
-            wscales[i, g] = sb("wscales%d%d" % (i, g), [P, N], U8)
-            nc.vector.quantize_mx(
-                out=codes[i, g][:].bitcast(FP8X4),
-                scales=wscales[i, g][:],
-                in_=grouped[:].rearrange("p m j -> p (m j)"),
-            )
+        nc.sync.dma_start(out=steer_sb[:], in_=steer)
+        load_weight(0, 1)
+        load_words(0, "words0")
+        load_weight(1, 1)
 
         picked_rows = sb("picked_rows", [P, S], U8)
         nc.vector.tensor_copy(out=picked_rows[:], in_=rows[:].indirect(offsets[:]))
-        for g, queue in enumerate((nc.scalar, nc.gpsimd)):
+
+        def place_scales(g):
             for r in range(4):
-                queue.dma_start(
+                nc.sync.dma_start(
                     out=planes[g][r:P:32, :].bitcast(I32),
                     in_=picked_rows[64 * g + 4 * r : 64 * (g + 1) : 16, :].bitcast(I32),
                 )
+
+        place_scales(0)
+        load_words(1, "rows")
+        place_scales(1)
+
+        codes, wscales = {}, {}
+
+        def quantize_weights(g, tag):
+            grouped = sb("grouped%d" % g, [P, 2, N, PACK], BF16)
+            for i in range(2):
+                nc.scalar.copy(
+                    out=grouped[:, i].rearrange("p (c i) j -> p c j i", i=4),
+                    in_=raw[i, g][:].rearrange("p j (c i) -> p c j i", i=4),
+                )
+            codes[g] = sb("codes%d" % g, [P, 2 * N], U32, tag=tag)
+            wscales[g] = sb("wscales%d" % g, [P, 2 * N], U8)
+            nc.vector.quantize_mx(
+                out=codes[g][:].bitcast(FP8X4),
+                scales=wscales[g][:],
+                in_=grouped[:].rearrange("p i m j -> p (i m j)"),
+            )
 
         picked = {}
 
@@ -109,23 +114,34 @@ def tile_picked_ymvdr_pow_p_kernel(tc, x_words, x_scales, w1, w2, steer, offs, o
                 in_=words[g][:].bitcast(U32).indirect(offsets[:, h * cols : (h + 1) * cols]),
             )
 
-        acc = {(i, h): bank("acc%d%d" % (i, h), "acc%d%d" % (i, h), [P, HALF]) for i in range(2) for h in range(2)}
+        spans = {(i, h): [(0, HALF)] for i in range(2) for h in range(2)}
+        spans[0, 1] = [(0, HALF // 2), (HALF // 2, HALF)]
+        acc = {
+            (i, h): [
+                bank("acc%d%d%d" % (i, h, n), "acc%d%d%d" % (i, h, n), [P, c1 - c0])
+                for n, (c0, c1) in enumerate(spans[i, h])
+            ]
+            for i in range(2)
+            for h in range(2)
+        }
 
         def multiply(i, g, h):
-            nc.tensor.matmul_mx(
-                out=acc[i, h][:],
-                lhsT=codes[i, g][:].bitcast(FP8X4),
-                lhsT_scale=wscales[i, g][:],
-                rhs=picked[g, h][:].bitcast(FP8X4),
-                rhs_scale=planes[g][:, h * HALF : (h + 1) * HALF],
-                start=(g == 0),
-                stop=(g == PASSES - 1),
-            )
+            for tile, (c0, c1) in zip(acc[i, h], spans[i, h]):
+                nc.tensor.matmul_mx(
+                    out=tile[:],
+                    lhsT=codes[g][:, i * N : (i + 1) * N].bitcast(FP8X4),
+                    lhsT_scale=wscales[g][:, i * N : (i + 1) * N],
+                    rhs=picked[g, h][:, c0:c1].bitcast(FP8X4),
+                    rhs_scale=planes[g][:, h * HALF + c0 : h * HALF + c1],
+                    start=(g == 0),
+                    stop=(g == PASSES - 1),
+                )
 
-        quantize_weight(0, 1)
-        quantize_weight(1, 1)
 
-        steer_t = bank("r3", "steer_t", [P, 2, VH])
+        gather_words(0, 0)
+        gather_words(0, 1)
+
+        steer_t = bank("r2", "steer_t", [P, 2, VH])
         for h in range(2):
             nc.tensor.transpose(steer_t[:, h, :], steer_sb[:, h * VH : (h + 1) * VH], ident[:])
         twice_s = sb("twice_s", [P, 2, VH])
@@ -135,11 +151,10 @@ def tile_picked_ymvdr_pow_p_kernel(tc, x_words, x_scales, w1, w2, steer, offs, o
             out=neg_s2[:], in0=steer_t[:], scalar=-0.5, in1=twice_s[:], op0=ALU.mult, op1=ALU.mult
         )
 
-        gather_words(0, 0)
-        gather_words(0, 1)
-        for i in range(2):
-            quantize_weight(i, 0)
-            for h in range(2):
+        quantize_weights(0, "words0")
+        quantize_weights(1, None)
+        for h in range(2):
+            for i in range(2):
                 multiply(i, 0, h)
 
         for h in range(2):
@@ -161,7 +176,7 @@ def tile_picked_ymvdr_pow_p_kernel(tc, x_words, x_scales, w1, w2, steer, offs, o
         def cross(ab, h, na, ds):
             nc.vector.scalar_tensor_tensor(
                 out=ab[:, ds, :],
-                in0=by_frame(acc[1, h])[:, ds, :],
+                in0=by_frame(acc[1, h][0])[:, ds, :],
                 scalar=0.25,
                 in1=na[:, ds, :],
                 op0=ALU.mult,
@@ -177,24 +192,25 @@ def tile_picked_ymvdr_pow_p_kernel(tc, x_words, x_scales, w1, w2, steer, offs, o
                 )
 
         every = slice(0, D)
-        nc.scalar.copy(out=na[0][:], in_=by_frame(acc[0, 0]))
-        nc.scalar.activation(out=bb[0][:], in_=by_frame(acc[1, 0]), func=ACT.Square, scale=0.5)
+        nc.scalar.copy(out=na[0][:], in_=by_frame(acc[0, 0][0]))
+        nc.scalar.activation(out=bb[0][:], in_=by_frame(acc[1, 0][0]), func=ACT.Square, scale=0.5)
         nc.vector.scalar_tensor_tensor(
-            out=aa[0][:], in0=by_frame(acc[0, 0]), scalar=0.25, in1=na[0][:], op0=ALU.mult, op1=ALU.mult
+            out=aa[0][:], in0=by_frame(acc[0, 0][0]), scalar=0.25, in1=na[0][:], op0=ALU.mult, op1=ALU.mult
         )
         cross(ab[0], 0, na[0], every)
-        nc.scalar.activation(out=bb[1][:], in_=by_frame(acc[1, 1]), func=ACT.Square, scale=0.5)
-        nc.scalar.copy(out=na[1][:], in_=by_frame(acc[0, 1]))
+        nc.scalar.activation(out=bb[1][:], in_=by_frame(acc[1, 1][0]), func=ACT.Square, scale=0.5)
+        nc.scalar.copy(out=na[1][:, :, 0 : VH // 2], in_=by_frame(acc[0, 1][0]))
+        nc.vector.tensor_copy(out=na[1][:, :, VH // 2 : VH], in_=by_frame(acc[0, 1][1]))
         maa0 = bank("r0", "maa0", [P, P])
         mbb0 = bank("r1", "mbb0", [P, P])
         mab0 = bank("r2", "mab0", [P, P])
         accumulate(mbb0, bb[0], every)
         accumulate(maa0, aa[0], every)
         accumulate(mab0, ab[0], every)
-        mbb1 = bank("acc00", "mbb1", [P, P])
+        mbb1 = bank("acc000", "mbb1", [P, P])
         accumulate(mbb1, bb[1], every)
-        mab1 = bank("acc10", "mab1", [P, P])
-        maa1 = bank("acc01", "maa1", [P, P])
+        mab1 = bank("acc100", "mab1", [P, P])
+        maa1 = bank("acc010", "maa1", [P, P])
         for ds in pairs:
             cross(ab[1], 1, na[1], ds)
             nc.scalar.activation(out=aa[1][:, ds, :], in_=na[1][:, ds, :], func=ACT.Square, scale=0.5)
@@ -207,12 +223,7 @@ def tile_picked_ymvdr_pow_p_kernel(tc, x_words, x_scales, w1, w2, steer, offs, o
             neg_ras2 = sb("neg_ras2%d" % h, [P, P])
             neg_rarb = sb("neg_rarb%d" % h, [P, P])
             rx2s = sb("rx2s%d" % h, [P, P])
-            if h == 0:
-                nc.vector.tensor_scalar(
-                    out=neg_rb[:], in0=mbb[:], scalar1=-1.0, scalar2=-0.1, op0=ALU.mult, op1=ALU.add
-                )
-            else:
-                nc.scalar.activation(out=neg_rb[:], in_=mbb[:], func=ACT.Copy, scale=-1.0, bias=-0.1)
+            nc.scalar.activation(out=neg_rb[:], in_=mbb[:], func=ACT.Copy, scale=-1.0, bias=-0.1)
             nc.vector.tensor_tensor(out=rx2s[:], in0=mab[:], in1=twice_s[:, h, :], op=ALU.mult)
             nc.scalar.activation(out=rx2[:], in_=mab[:], func=ACT.Square)
             nc.vector.scalar_tensor_tensor(
@@ -235,5 +246,5 @@ def tile_picked_ymvdr_pow_p_kernel(tc, x_words, x_scales, w1, w2, steer, offs, o
             nc.vector.tensor_tensor(out=result[:], in0=ln_num[:], in1=ln_den[:], op=ALU.subtract)
             nc.sync.dma_start(out=out[:, h * VH : (h + 1) * VH], in_=result[:])
 
-        finish(0, maa0, mbb0, mab0, "r3", "r1")
-        finish(1, maa1, mbb1, mab1, "acc11", "r2")
+        finish(0, maa0, mbb0, mab0, "acc011", "acc110")
+        finish(1, maa1, mbb1, mab1, "r2", "r1")

from contextlib import ExitStack

import concourse.mybir as mybir
from concourse.masks import make_identity

K, T, S, N, D, V = 1024, 4096, 1024, 128, 4, 256
FLOPS = 2 * 2 * K * N * S

F32 = mybir.dt.float32
BF16 = mybir.dt.bfloat16
I32 = mybir.dt.int32
U32 = mybir.dt.uint32
U16 = mybir.dt.uint16
U8 = mybir.dt.uint8
FP8X4 = mybir.dt.float8_e4m3fn_x4
ACT = mybir.ActivationFunctionType
ALU = mybir.AluOpType

P = 128
PACK = 4
K_PASS = P * PACK
PASSES = K // K_PASS
HALF = S // 2
VH = HALF // D
CLEAR = 2048


def tile_picked_ymvdr_pow_p_kernel(tc, x_words, x_scales, w1, w2, steer, offs, out):
    nc = tc.nc
    with ExitStack() as ctx:
        keep = ctx.enter_context(tc.tile_pool(name="keep", bufs=1))
        psum = ctx.enter_context(tc.psum_pool(name="psum", bufs=1))

        def sb(name, shape, dtype=F32, tag=None):
            return keep.tile(shape, dtype, name=name, tag=tag or name, align_bytes=64)

        def bank(tag, name, shape):
            return psum.tile(shape, F32, name=name, tag=tag)

        offsets = keep.tile([P, S // 16], U16, name="offsets")
        words = {}
        rows = sb("rows", [P, T], U8)
        planes = [sb("planes%d" % g, [P, S], U8) for g in range(PASSES)]
        raw = {(i, g): sb("raw%d%d" % (i, g), [P, PACK, N]) for i in range(2) for g in range(PASSES)}
        steer_sb = sb("steer_sb", [P, V])
        ident = sb("ident", [P, P])

        def load_words(g, tag):
            words[g] = sb("words%d" % g, [P, T], I32, tag=tag)
            nc.sync.dma_start(out=words[g][:], in_=x_words[g].rearrange("p c r -> p (c r)").bitcast(I32))

        def load_weight(i, g):
            rows = (w1, w2)[i][g * K_PASS : (g + 1) * K_PASS, :]
            nc.sync.dma_start(out=raw[i, g][:], in_=rows.rearrange("(p j) m -> p j m", j=PACK))

        nc.gpsimd.memset(rows[:, 0:CLEAR].bitcast(I32), 0)
        nc.vector.memset(rows[:, CLEAR:T].bitcast(I32), 0)
        for g in range(PASSES):
            nc.vector.memset(planes[g][:].bitcast(I32), 0)
        make_identity(nc, ident[:])
        ones = sb("ones", [P, 1])
        nc.gpsimd.memset(ones[:], 1.0)
        warm = sb("warm", [P, 1])
        nc.scalar.activation(out=warm[:], in_=ones[:], func=ACT.Ln)
        nc.sync.dma_start(offsets[:], offs)
        load_weight(0, 0)
        load_weight(1, 0)
        nc.sync.dma_start(
            out=rows[0:P:4, :].bitcast(I32), in_=x_scales.rearrange("g q t -> (g q) t").bitcast(I32)
        )
        nc.sync.dma_start(out=steer_sb[:], in_=steer)
        load_weight(0, 1)
        load_words(0, "words0")
        load_weight(1, 1)

        picked_rows = sb("picked_rows", [P, S], U8)
        nc.vector.tensor_copy(out=picked_rows[:], in_=rows[:].indirect(offsets[:]))

        def place_scales(g):
            for r in range(4):
                nc.sync.dma_start(
                    out=planes[g][r:P:32, :].bitcast(I32),
                    in_=picked_rows[64 * g + 4 * r : 64 * (g + 1) : 16, :].bitcast(I32),
                )

        place_scales(0)
        load_words(1, "rows")
        place_scales(1)

        codes, wscales = {}, {}

        def quantize_weights(g, tag):
            grouped = sb("grouped%d" % g, [P, 2, N, PACK], BF16)
            for i in range(2):
                nc.scalar.copy(
                    out=grouped[:, i].rearrange("p (c i) j -> p c j i", i=4),
                    in_=raw[i, g][:].rearrange("p j (c i) -> p c j i", i=4),
                )
            codes[g] = sb("codes%d" % g, [P, 2 * N], U32, tag=tag)
            wscales[g] = sb("wscales%d" % g, [P, 2 * N], U8)
            nc.vector.quantize_mx(
                out=codes[g][:].bitcast(FP8X4),
                scales=wscales[g][:],
                in_=grouped[:].rearrange("p i m j -> p (i m j)"),
            )

        picked = {}

        def gather_words(g, h):
            picked[g, h] = sb("picked%d%d" % (g, h), [P, HALF], U32)
            cols = HALF // 16
            nc.vector.tensor_copy(
                out=picked[g, h][:],
                in_=words[g][:].bitcast(U32).indirect(offsets[:, h * cols : (h + 1) * cols]),
            )

        spans = {(i, h): [(0, HALF)] for i in range(2) for h in range(2)}
        spans[0, 1] = [(0, HALF // 2), (HALF // 2, HALF)]
        acc = {
            (i, h): [
                bank("acc%d%d%d" % (i, h, n), "acc%d%d%d" % (i, h, n), [P, c1 - c0])
                for n, (c0, c1) in enumerate(spans[i, h])
            ]
            for i in range(2)
            for h in range(2)
        }

        def multiply(i, g, h):
            for tile, (c0, c1) in zip(acc[i, h], spans[i, h]):
                nc.tensor.matmul_mx(
                    out=tile[:],
                    lhsT=codes[g][:, i * N : (i + 1) * N].bitcast(FP8X4),
                    lhsT_scale=wscales[g][:, i * N : (i + 1) * N],
                    rhs=picked[g, h][:, c0:c1].bitcast(FP8X4),
                    rhs_scale=planes[g][:, h * HALF + c0 : h * HALF + c1],
                    start=(g == 0),
                    stop=(g == PASSES - 1),
                )


        gather_words(0, 0)
        gather_words(0, 1)

        steer_t = bank("r2", "steer_t", [P, 2, VH])
        for h in range(2):
            nc.tensor.transpose(steer_t[:, h, :], steer_sb[:, h * VH : (h + 1) * VH], ident[:])
        twice_s = sb("twice_s", [P, 2, VH])
        nc.scalar.activation(out=twice_s[:], in_=steer_t[:], func=ACT.Copy, scale=2.0)
        neg_s2 = sb("neg_s2", [P, 2, VH])
        nc.vector.scalar_tensor_tensor(
            out=neg_s2[:], in0=steer_t[:], scalar=-0.5, in1=twice_s[:], op0=ALU.mult, op1=ALU.mult
        )

        quantize_weights(0, "words0")
        quantize_weights(1, None)
        for h in range(2):
            for i in range(2):
                multiply(i, 0, h)

        for h in range(2):
            gather_words(1, h)
            for i in ((0, 1), (1, 0))[h]:
                multiply(i, 1, h)

        def by_frame(tile):
            return tile[:].rearrange("p (v d) -> p d v", d=D)

        def transpose_sum(dst, terms):
            for n, term in enumerate(terms):
                nc.tensor.matmul(
                    dst[:], lhsT=term, rhs=ident[:], is_transpose=True, start=(n == 0), stop=(n == len(terms) - 1)
                )

        pairs = [slice(0, 2), slice(2, 4)]

        def cross(ab, h, na, ds):
            nc.vector.scalar_tensor_tensor(
                out=ab[:, ds, :],
                in0=by_frame(acc[1, h][0])[:, ds, :],
                scalar=0.25,
                in1=na[:, ds, :],
                op0=ALU.mult,
                op1=ALU.mult,
            )

        na, aa, bb, ab = [[sb("%s%d" % (name, h), [P, D, VH]) for h in range(2)] for name in ("na", "aa", "bb", "ab")]

        def accumulate(dst, tile, ds):
            for d in range(ds.start, ds.stop):
                nc.tensor.matmul(
                    dst[:], lhsT=tile[:, d, :], rhs=ident[:], is_transpose=True, start=(d == 0), stop=(d == D - 1)
                )

        every = slice(0, D)
        nc.scalar.copy(out=na[0][:], in_=by_frame(acc[0, 0][0]))
        nc.scalar.activation(out=bb[0][:], in_=by_frame(acc[1, 0][0]), func=ACT.Square, scale=0.5)
        nc.vector.scalar_tensor_tensor(
            out=aa[0][:], in0=by_frame(acc[0, 0][0]), scalar=0.25, in1=na[0][:], op0=ALU.mult, op1=ALU.mult
        )
        cross(ab[0], 0, na[0], every)
        nc.scalar.activation(out=bb[1][:], in_=by_frame(acc[1, 1][0]), func=ACT.Square, scale=0.5)
        nc.scalar.copy(out=na[1][:, :, 0 : VH // 2], in_=by_frame(acc[0, 1][0]))
        nc.vector.tensor_copy(out=na[1][:, :, VH // 2 : VH], in_=by_frame(acc[0, 1][1]))
        maa0 = bank("r0", "maa0", [P, P])
        mbb0 = bank("r1", "mbb0", [P, P])
        mab0 = bank("r2", "mab0", [P, P])
        accumulate(mbb0, bb[0], every)
        accumulate(maa0, aa[0], every)
        accumulate(mab0, ab[0], every)
        mbb1 = bank("acc000", "mbb1", [P, P])
        accumulate(mbb1, bb[1], every)
        mab1 = bank("acc100", "mab1", [P, P])
        maa1 = bank("acc010", "maa1", [P, P])
        for ds in pairs:
            cross(ab[1], 1, na[1], ds)
            nc.scalar.activation(out=aa[1][:, ds, :], in_=na[1][:, ds, :], func=ACT.Square, scale=0.5)
            accumulate(mab1, ab[1], ds)
            accumulate(maa1, aa[1], ds)

        def finish(h, maa, mbb, mab, num_tag, den_tag):
            neg_rb = sb("neg_rb%d" % h, [P, P])
            rx2 = sb("rx2%d" % h, [P, P])
            neg_ras2 = sb("neg_ras2%d" % h, [P, P])
            neg_rarb = sb("neg_rarb%d" % h, [P, P])
            rx2s = sb("rx2s%d" % h, [P, P])
            nc.scalar.activation(out=neg_rb[:], in_=mbb[:], func=ACT.Copy, scale=-1.0, bias=-0.1)
            nc.vector.tensor_tensor(out=rx2s[:], in0=mab[:], in1=twice_s[:, h, :], op=ALU.mult)
            nc.scalar.activation(out=rx2[:], in_=mab[:], func=ACT.Square)
            nc.vector.scalar_tensor_tensor(
                out=neg_rarb[:], in0=maa[:], scalar=0.1, in1=neg_rb[:], op0=ALU.add, op1=ALU.mult
            )
            nc.vector.scalar_tensor_tensor(
                out=neg_ras2[:], in0=maa[:], scalar=0.1, in1=neg_s2[:, h, :], op0=ALU.add, op1=ALU.mult
            )
            neg_num = bank(num_tag, "neg_num%d" % h, [P, VH])
            neg_den = bank(den_tag, "neg_den%d" % h, [P, VH])
            terms = [(neg_den, neg_rb, True, False), (neg_den, rx2s, False, False), (neg_num, rx2, True, False),
                     (neg_num, neg_rarb, False, True), (neg_den, neg_ras2, False, True)]
            for dst, term, first, last in terms:
                nc.tensor.matmul(dst[:], lhsT=term[:], rhs=ident[:], is_transpose=True, start=first, stop=last)
            ln_num = sb("ln_num%d" % h, [P, VH])
            ln_den = sb("ln_den%d" % h, [P, VH])
            nc.scalar.activation(out=ln_num[:], in_=neg_num[:], func=ACT.Ln, scale=-1.0, bias=0.02)
            nc.scalar.activation(out=ln_den[:], in_=neg_den[:], func=ACT.Ln, scale=-1.0, bias=0.05)
            result = sb("result%d" % h, [P, VH])
            nc.vector.tensor_tensor(out=result[:], in0=ln_num[:], in1=ln_den[:], op=ALU.subtract)
            nc.sync.dma_start(out=out[:, h * VH : (h + 1) * VH], in_=result[:])

        finish(0, maa0, mbb0, mab0, "acc011", "acc110")
        finish(1, maa1, mbb1, mab1, "r2", "r1")
